import numpy as np
import ml_dtypes


def mxq(x, axis, fmt="e4m3"):
    dtype, down = {"e4m3": (ml_dtypes.float8_e4m3fn, 7), "e5m2": (ml_dtypes.float8_e5m2, 14)}[fmt]
    v = np.moveaxis(np.asarray(x, np.float32).astype(ml_dtypes.bfloat16).astype(np.float64), axis, -1)
    blocks = v.reshape(v.shape[:-1] + (-1, 32))
    amax = np.abs(blocks).max(-1, keepdims=True)
    byte = np.maximum(np.where(amax > 0, np.frexp(amax)[1] - 1 + 127, 0) - down, 1)
    scale = np.exp2(byte - 127.0)
    codes = (blocks / scale).astype(np.float32).astype(dtype).astype(np.float64)
    return np.moveaxis((codes * scale).reshape(v.shape), -1, axis)


WIDE = False


def mx_kscale(k):
    if not WIDE:
        return np.ones(k)
    levels = np.array([30, -30])
    if k % 512:
        return np.exp2(np.random.permutation(np.resize(levels, k // 32))).repeat(32)
    a = np.empty((k // 512, 16))
    for p in range(k // 512):
        a[p, :8] = np.random.permutation(np.resize(levels, 8))
        for g in range(8):
            far = levels[np.abs(levels - a[p, g]) >= 10]
            a[p, g + 8] = far[np.random.randint(len(far))]
    return np.exp2(a.ravel()).repeat(32)


def f64(x):
    return np.asarray(x).astype(np.float64)


def striped(idx):
    return np.tile(np.asarray(idx).reshape(-1, 16).T, (8, 1)).astype(np.uint16)


def unstriped(offs):
    return offs[:16].T.reshape(-1).astype(np.int64)


E2M1 = np.array([0.0, 0.5, 1.0, 1.5, 2.0, 3.0, 4.0, 6.0, -0.0, -0.5, -1.0, -1.5, -2.0, -3.0, -4.0, -6.0])


def pack_weight(w, fmt):
    k, n = w.shape
    w = f64(np.asarray(w, np.float32).astype(ml_dtypes.bfloat16)).reshape(k // 32, 32, n)
    amax = np.abs(w).max(1)
    if fmt in ("e4m3", "e5m2"):
        byte = np.frexp(amax)[1] - 1 + 127 - (7 if fmt == "e4m3" else 14)
    else:
        mant, ex = np.frexp(amax / 6.0)
        byte = np.where(mant > 0.5, ex, ex - 1) + 127
    byte = np.clip(np.where(amax > 0, byte, 1), 1, 254)
    scaled = (w * np.exp2(127.0 - byte)[:, None, :]).reshape(k, n).astype(np.float32)
    by_word = np.ascontiguousarray(scaled.reshape(k // 512, 128, 4, n).transpose(0, 1, 3, 2))
    if fmt in ("e4m3", "e5m2"):
        words = by_word.astype(ml_dtypes.float8_e4m3fn if fmt == "e4m3" else ml_dtypes.float8_e5m2).view(np.uint8)
    else:
        c = by_word.astype(ml_dtypes.float4_e2m1fn).view(np.uint8) & 0xF
        words = (c[..., 0::2] | (c[..., 1::2] << 4)).reshape(k // 512, 128, 2 * n)
    return np.ascontiguousarray(words), np.ascontiguousarray(byte.astype(np.uint8).reshape(k // 512, 16, n))


def unpack_weight(words, scales, fmt):
    g, _, n = scales.shape
    words = np.ascontiguousarray(words).reshape(g, 128, n, -1)
    if fmt in ("e4m3", "e5m2"):
        vals = words.view(ml_dtypes.float8_e4m3fn if fmt == "e4m3" else ml_dtypes.float8_e5m2).astype(np.float64)
    else:
        nib = np.empty((g, 128, n, 4), np.uint8)
        nib[..., 0::2] = words & 0xF
        nib[..., 1::2] = words >> 4
        vals = E2M1[nib]
    vals = vals * np.repeat(np.exp2(scales.astype(np.float64) - 127.0), 8, axis=1)[..., None]
    return vals.transpose(0, 1, 3, 2).reshape(g * 512, n)


def sigmoid(v):
    return 1.0 / (1.0 + np.exp(-v))


def sgn(shape):
    return np.random.uniform(0.5, 2.0, shape) * np.where(np.random.standard_normal(shape) < 0, -1.0, 1.0)


K, T, J, R, F, Z, O, N, E = 512, 1024, 256, 512, 512, 1024, 128, 256, 512


def setup_inputs():
    n = np.random.standard_normal
    idx = np.random.permutation(T)[:J]
    idx2 = np.random.permutation(Z)[:J]
    idx3 = np.random.permutation(J)[:O]
    idx4 = np.random.permutation(J)[:O]
    idx5 = np.random.permutation(J)[:O]
    idx6 = np.random.permutation(E)[:O]
    idx7 = np.random.permutation(E)[:O]
    fk = mx_kscale(K)
    ff = mx_kscale(F)
    fr = mx_kscale(R)
    xtp = pack_weight(n((K, T)) / fk[:, None], "e5m2")
    xop = pack_weight(n((F, Z)) / ff[:, None], "e4m3")
    wp = pack_weight(n((K, R)) * 1 / np.sqrt(K) * fk[:, None], "e2m1")
    w0p = pack_weight(n((F, R)) * 1 / np.sqrt(F) * ff[:, None], "e2m1")
    wbp = pack_weight(n((R, N)) * 1 / np.sqrt(R) / fr[:, None], "e2m1")
    return {
        "xt_words": xtp[0],
        "xt_scales": xtp[1],
        "xo_words": xop[0],
        "xo_scales": xop[1],
        "w_words": wp[0],
        "w_scales": wp[1],
        "w0_words": w0p[0],
        "w0_scales": w0p[1],
        "sa": (np.random.uniform(0.5, 1.6, (R, 1)) * fr[:, None]).astype(np.float32),
        "sb": (np.random.uniform(0.5, 1.6, (R, 1)) * fr[:, None]).astype(np.float32),
        "sg": (sgn((R, 1))).astype(np.float32),
        "bg": (np.random.uniform(-2.0, 2.0, (R, 1))).astype(np.float32),
        "wb_words": wbp[0],
        "wb_scales": wbp[1],
        "offs": striped(idx),
        "offs2": striped(idx2),
        "offs3": striped(idx3),
        "offs4": striped(idx4),
        "offs5": striped(idx5),
        "offs6": striped(idx6),
        "offs7": striped(idx7),
    }


def reference(xt_words, xt_scales, xo_words, xo_scales, w_words, w_scales, w0_words, w0_scales, sa, sb, sg, bg, wb_words, wb_scales, offs, offs2, offs3, offs4, offs5, offs6, offs7):
    idx = unstriped(offs)
    idx2 = unstriped(offs2)
    idx3 = unstriped(offs3)
    idx4 = unstriped(offs4)
    idx5 = unstriped(offs5)
    idx6 = unstriped(offs6)
    idx7 = unstriped(offs7)
    xtu = unpack_weight(xt_words, xt_scales, "e5m2")
    xou = unpack_weight(xo_words, xo_scales, "e4m3")
    wu = unpack_weight(w_words, w_scales, "e2m1")
    w0u = unpack_weight(w0_words, w0_scales, "e2m1")
    wbu = unpack_weight(wb_words, wb_scales, "e2m1")
    xtidxg = xtu[:, idx]
    xoidx2g = xou[:, idx2]
    a = wu.T @ xtidxg + w0u.T @ xoidx2g
    hid = np.abs(a[:, idx3] * f64(sa) * sigmoid(a[:, idx4] * f64(sg) + f64(bg)) - a[:, idx5] * f64(sb))
    hidq = mxq(hid, 0, "e4m3")
    p = wbu.T @ hidq
    pa = np.zeros((N, E))
    pa[:, idx6] = p
    pb = np.zeros((N, E))
    pb[:, idx7] = p
    y = pa + pb
    return y

@@ -1,0 +1,147 @@
+from contextlib import ExitStack
+
+import concourse.mybir as mybir
+
+F32 = mybir.dt.float32
+BF16 = mybir.dt.bfloat16
+I32 = mybir.dt.int32
+U32 = mybir.dt.uint32
+U16 = mybir.dt.uint16
+U8 = mybir.dt.uint8
+E4M3 = mybir.dt.float8_e4m3fn_x4
+E5M2 = mybir.dt.float8_e5m2_x4
+E2M1 = mybir.dt.float4_e2m1fn_x4
+ACT = mybir.ActivationFunctionType
+ALU = mybir.AluOpType
+
+P = 128
+PACK = 4
+QUADS = 4
+T, J, R, O, N, E = 1024, 256, 512, 128, 256, 512
+FLOPS = 2 * (2 * 512 * R * J + R * N * O)
+
+
+def tile_list_gatedless_bank_one_pagetwice_kernel(tc, xt_words, xt_scales, xo_words, xo_scales, w_words, w_scales, w0_words, w0_scales, sa, sb, sg, bg, wb_words, wb_scales, offs, offs2, offs3, offs4, offs5, offs6, offs7, out):
+    nc = tc.nc
+    with ExitStack() as ctx:
+        held = ctx.enter_context(tc.tile_pool(name="held", bufs=1))
+        psum = ctx.enter_context(tc.psum_pool(name="psum", bufs=1))
+
+        def load_list(src, name):
+            tile = held.tile(list(src.shape), U16, name=name)
+            nc.sync.dma_start(tile[:], src)
+            return tile
+
+        def load_rows(engine, plane, scales):
+            for r in range(PACK):
+                engine.dma_start(plane[r:P:32, :].bitcast(I32), scales[0][r:16:PACK, :].bitcast(I32))
+
+        xt_plane = held.tile([P, T], U8, name="xt_plane", align_bytes=64)
+        xo_plane = held.tile([P, T], U8, name="xo_plane", align_bytes=64)
+        w_plane = held.tile([P, 2, R], U8, name="w_plane", align_bytes=64)
+        wb_plane = held.tile([P, N], U8, name="wb_plane", align_bytes=64)
+        nc.vector.memset(xo_plane[:].bitcast(I32), 0)
+        nc.vector.memset(xt_plane[:].bitcast(I32), 0)
+        nc.vector.memset(w_plane[:].rearrange("p a r -> p (a r)").bitcast(I32), 0)
+        nc.vector.memset(wb_plane[:].bitcast(I32), 0)
+
+        xt_rows = held.tile([PACK, QUADS, T // 4], I32, name="xt_rows")
+        w_rows = held.tile([PACK, QUADS, 2, R // 4], I32, name="w_rows")
+        xt_table = held.tile([P, T], U32, name="xt_table")
+        xo_table = held.tile([P, T], U32, name="xo_table")
+        w_raw = held.tile([P, 2 * R], U8, name="w_raw")
+        w0_raw = held.tile([P, 2 * R], U8, name="w0_raw")
+        nc.scalar.dma_start(xt_rows[:], xt_scales[0].bitcast(I32).rearrange("(q r) c -> r q c", r=PACK))
+        for a, scales in enumerate((w_scales, w0_scales)):
+            nc.scalar.dma_start(w_rows[:, :, a, :], scales[0].bitcast(I32).rearrange("(q r) c -> r q c", r=PACK))
+        nc.scalar.dma_start(w0_raw[:].bitcast(I32), w0_words[0].bitcast(I32))
+        load_rows(nc.scalar, xo_plane, xo_scales)
+        l1 = load_list(offs, "l1")
+        l2 = load_list(offs2, "l2")
+        nc.sync.dma_start(w_raw[:].bitcast(I32), w_words[0].bitcast(I32))
+        nc.sync.dma_start(xt_table[:].bitcast(I32), xt_words[0].rearrange("p n t -> p (n t)").bitcast(I32))
+        nc.sync.dma_start(xo_table[:].bitcast(I32), xo_words[0].rearrange("p n t -> p (n t)").bitcast(I32))
+        l4 = load_list(offs4, "l4")
+        l3 = load_list(offs3, "l3")
+        l5 = load_list(offs5, "l5")
+        rows = {}
+        for name, src in (("sg", sg), ("bg", bg), ("sa", sa), ("sb", sb)):
+            rows[name] = held.tile([P, PACK], F32, name=name)
+            nc.gpsimd.dma_start(rows[name][:], src.rearrange("(p t) one -> p (t one)", t=PACK))
+        wb_codes = held.tile([P, 2 * N], U8, name="wb_codes", align_bytes=64)
+        l6 = load_list(offs6, "l6")
+        l7 = load_list(offs7, "l7")
+        nc.sync.dma_start(wb_codes[:].bitcast(I32), wb_words[0].bitcast(I32))
+        load_rows(nc.sync, wb_plane, wb_scales)
+
+        pages = [[held.tile([P, E], F32, name="page%d%d" % (a, h)) for h in range(2)] for a in range(2)]
+        for a in range(2):
+            for h in range(2):
+                nc.vector.memset(pages[a][h][:], 0.0)
+
+        w_codes = [held.tile([P, PACK, 2 * P], U8, name="w_codes%d" % a, align_bytes=64) for a in range(2)]
+        for a, raw in enumerate((w_raw, w0_raw)):
+            nc.scalar.copy(w_codes[a][:].bitcast(U16), raw[:].bitcast(U16).rearrange("p (m t) -> p t m", t=PACK))
+
+        xt_gs = held.tile([P, J], U8, name="xt_gs", align_bytes=64)
+        xo_gs = held.tile([P, J], U8, name="xo_gs", align_bytes=64)
+        xt_g = held.tile([P, J], U32, name="xt_g", align_bytes=64)
+        xo_g = held.tile([P, J], U32, name="xo_g", align_bytes=64)
+        for q in range(QUADS):
+            nc.vector.tensor_copy(xt_plane[32 * q : 32 * q + PACK, :].bitcast(I32), xt_rows[:, q, :])
+        w_plane_words = w_plane[:].rearrange("p a r -> p (a r)").bitcast(I32)
+        for q in range(QUADS):
+            nc.vector.tensor_copy(w_plane_words[32 * q : 32 * q + PACK, :], w_rows[:, q, :, :].rearrange("r a c -> r (a c)"))
+        nc.vector.tensor_copy(xt_gs[:], xt_plane[:].indirect(l1[:]))
+        nc.vector.tensor_copy(xt_g[:], xt_table[:].indirect(l1[:]))
+        nc.vector.tensor_copy(xo_gs[:], xo_plane[:].indirect(l2[:]))
+        nc.vector.tensor_copy(xo_g[:], xo_table[:].indirect(l2[:]))
+        w_dealt = [held.tile([P, 2, P], U8, name="w_dealt%d" % t, align_bytes=64) for t in range(PACK)]
+        for t in range(PACK):
+            nc.gpsimd.tensor_copy(w_dealt[t][:], w_plane[:].rearrange("p a (m t) -> p t a m", t=PACK)[:, t, :, :])
+
+        acc = [psum.tile([P, J], F32, name="acc%d" % t) for t in range(PACK)]
+        for a, (codes, scales, fmt) in enumerate(((xt_g, xt_gs, E5M2), (xo_g, xo_gs, E4M3))):
+            for t in range(PACK):
+                nc.tensor.matmul_mx(out=acc[t][:], lhsT=w_codes[a][:, t, :].bitcast(E2M1), lhsT_scale=w_dealt[t][:, a, :],
+                                    rhs=codes[:].bitcast(fmt), rhs_scale=scales[:], start=(a == 0), stop=(a == 1))
+
+        hid = held.tile([P, O, PACK], BF16, name="hid", align_bytes=64)
+        a_rows = [held.tile([P, J], F32, name="a_rows%d" % t) for t in range(PACK)]
+        for t in range(PACK):
+            nc.vector.tensor_copy(a_rows[t][:], acc[t][:])
+        for t in range(PACK):
+            gate = held.tile([P, O], F32, name="gate%d" % t)
+            first = held.tile([P, O], F32, name="first%d" % t)
+            second = held.tile([P, O], F32, name="second%d" % t)
+            gated = held.tile([P, O], F32, name="gated%d" % t)
+            diff = held.tile([P, O], F32, name="diff%d" % t)
+            nc.scalar.activation(out=gate[:], in_=a_rows[t][:].indirect(l4[:]), func=ACT.Sigmoid, bias=rows["bg"][:, t : t + 1], scale=rows["sg"][:, t : t + 1])
+            nc.scalar.activation(out=first[:], in_=a_rows[t][:].indirect(l3[:]), func=ACT.Copy, scale=rows["sa"][:, t : t + 1])
+            nc.scalar.activation(out=second[:], in_=a_rows[t][:].indirect(l5[:]), func=ACT.Copy, scale=rows["sb"][:, t : t + 1])
+            nc.vector.tensor_tensor(gated[:], first[:], gate[:], ALU.mult)
+            nc.vector.tensor_tensor(diff[:], gated[:], second[:], ALU.subtract)
+            nc.vector.scalar_tensor_tensor(hid[:, :, t], diff[:], -1.0, diff[:], ALU.mult, ALU.max)
+
+        hid_codes = held.tile([P, O], U32, name="hid_codes", align_bytes=64)
+        hid_scales = held.tile([P, O], U8, name="hid_scales", align_bytes=64)
+        nc.vector.quantize_mx(out=hid_codes[:].bitcast(E4M3), scales=hid_scales[:], in_=hid[:].rearrange("p o t -> p (o t)"))
+
+        prod = [psum.tile([P, O], F32, name="prod%d" % h) for h in range(2)]
+        p_rows = [held.tile([P, O], F32, name="p_rows%d" % h) for h in range(2)]
+        for h in range(2):
+            nc.tensor.matmul_mx(out=prod[h][:], lhsT=wb_codes[:, 2 * P * h : 2 * P * (h + 1)].bitcast(E2M1), lhsT_scale=wb_plane[:, P * h : P * (h + 1)],
+                                rhs=hid_codes[:].bitcast(E4M3), rhs_scale=hid_scales[:], start=True, stop=True)
+        nc.vector.tensor_copy(p_rows[0][:], prod[0][:])
+        nc.scalar.copy(p_rows[1][:], prod[1][:])
+        sums = [held.tile([P, E], F32, name="sums%d" % h) for h in range(2)]
+        half = O // 32
+        nc.vector.tensor_copy(pages[0][0][:].indirect(l6[:]), p_rows[0][:])
+        nc.scalar.activation(out=pages[1][0][:].indirect(l7[:]), in_=p_rows[0][:], func=ACT.Copy)
+        nc.scalar.activation(out=pages[0][1][:].indirect(l6[:, half:]), in_=p_rows[1][:, O // 2 :], func=ACT.Copy)
+        nc.scalar.activation(out=pages[1][1][:].indirect(l7[:]), in_=p_rows[1][:], func=ACT.Copy)
+        nc.vector.tensor_tensor(sums[0][:], pages[0][0][:], pages[1][0][:], ALU.add)
+        nc.sync.dma_start(out[0:P, :], sums[0][:])
+        nc.vector.tensor_copy(pages[0][1][:].indirect(l6[:, :half]), p_rows[1][:, : O // 2])
+        nc.vector.tensor_tensor(sums[1][:], pages[0][1][:], pages[1][1][:], ALU.add)
+        nc.sync.dma_start(out[P : 2 * P, :], sums[1][:])

@@ -36,32 +36,36 @@ def tile_list_gatedless_bank_one_pagetwice_kernel(tc, xt_words, xt_scales, xo_wo
             for r in range(PACK):
                 engine.dma_start(plane[r:P:32, :].bitcast(I32), scales[0][r:16:PACK, :].bitcast(I32))
 
+        def load_halves(engines, stage, scales):
+            rows4 = scales[0].bitcast(I32).rearrange("(h q r) c -> q r h c", h=2, q=2)
+            for q in range(2):
+                engines[q].dma_start(stage[32 * q : 32 * q + PACK], rows4[q])
+
+        xt_stage = held.tile([64, 2, T // 4], I32, name="xt_stage")
+        w_stage = held.tile([64, 2, 2, R // 4], I32, name="w_stage")
         xt_plane = held.tile([P, T], U8, name="xt_plane", align_bytes=64)
         xo_plane = held.tile([P, T], U8, name="xo_plane", align_bytes=64)
-        w_plane = held.tile([P, 2, R], U8, name="w_plane", align_bytes=64)
         wb_plane = held.tile([P, N], U8, name="wb_plane", align_bytes=64)
+        nc.vector.memset(xt_stage[:], 0)
         nc.vector.memset(xo_plane[:].bitcast(I32), 0)
-        nc.vector.memset(xt_plane[:].bitcast(I32), 0)
-        nc.vector.memset(w_plane[:].rearrange("p a r -> p (a r)").bitcast(I32), 0)
+        nc.vector.memset(w_stage[:], 0)
         nc.vector.memset(wb_plane[:].bitcast(I32), 0)
 
-        xt_rows = held.tile([PACK, QUADS, T // 4], I32, name="xt_rows")
-        w_rows = held.tile([PACK, QUADS, 2, R // 4], I32, name="w_rows")
         xt_table = held.tile([P, T], U32, name="xt_table")
-        xo_table = held.tile([P, T], U32, name="xo_table")
+        xo_table = held.tile([P, T], U32, name="xo_table", tag="xo_table")
         w_raw = held.tile([P, 2 * R], U8, name="w_raw")
         w0_raw = held.tile([P, 2 * R], U8, name="w0_raw")
-        nc.scalar.dma_start(xt_rows[:], xt_scales[0].bitcast(I32).rearrange("(q r) c -> r q c", r=PACK))
-        for a, scales in enumerate((w_scales, w0_scales)):
-            nc.scalar.dma_start(w_rows[:, :, a, :], scales[0].bitcast(I32).rearrange("(q r) c -> r q c", r=PACK))
+        nc.scalar.dma_start(w_raw[:].bitcast(I32), w_words[0].bitcast(I32))
         nc.scalar.dma_start(w0_raw[:].bitcast(I32), w0_words[0].bitcast(I32))
-        load_rows(nc.scalar, xo_plane, xo_scales)
+        nc.scalar.dma_start(xt_table[:].bitcast(I32), xt_words[0].rearrange("p n t -> p (n t)").bitcast(I32))
         l1 = load_list(offs, "l1")
         l2 = load_list(offs2, "l2")
-        nc.sync.dma_start(w_raw[:].bitcast(I32), w_words[0].bitcast(I32))
-        nc.sync.dma_start(xt_table[:].bitcast(I32), xt_words[0].rearrange("p n t -> p (n t)").bitcast(I32))
-        nc.sync.dma_start(xo_table[:].bitcast(I32), xo_words[0].rearrange("p n t -> p (n t)").bitcast(I32))
         l4 = load_list(offs4, "l4")
+        load_halves((nc.sync, nc.sync), xt_stage[:], xt_scales)
+        load_rows(nc.sync, xo_plane, xo_scales)
+        nc.sync.dma_start(xo_table[:].bitcast(I32), xo_words[0].rearrange("p n t -> p (n t)").bitcast(I32))
+        load_halves((nc.sync, nc.sync), w_stage[:, :, 0, :], w_scales)
+        load_halves((nc.sync, nc.sync), w_stage[:, :, 1, :], w0_scales)
         l3 = load_list(offs3, "l3")
         l5 = load_list(offs5, "l5")
         rows = {}
@@ -87,45 +91,50 @@ def tile_list_gatedless_bank_one_pagetwice_kernel(tc, xt_words, xt_scales, xo_wo
         xo_gs = held.tile([P, J], U8, name="xo_gs", align_bytes=64)
         xt_g = held.tile([P, J], U32, name="xt_g", align_bytes=64)
         xo_g = held.tile([P, J], U32, name="xo_g", align_bytes=64)
-        for q in range(QUADS):
-            nc.vector.tensor_copy(xt_plane[32 * q : 32 * q + PACK, :].bitcast(I32), xt_rows[:, q, :])
-        w_plane_words = w_plane[:].rearrange("p a r -> p (a r)").bitcast(I32)
-        for q in range(QUADS):
-            nc.vector.tensor_copy(w_plane_words[32 * q : 32 * q + PACK, :], w_rows[:, q, :, :].rearrange("r a c -> r (a c)"))
+        for h in range(2):
+            nc.vector.tensor_copy(xt_plane[64 * h : 64 * (h + 1), :].bitcast(I32), xt_stage[:, h, :])
         nc.vector.tensor_copy(xt_gs[:], xt_plane[:].indirect(l1[:]))
         nc.vector.tensor_copy(xt_g[:], xt_table[:].indirect(l1[:]))
         nc.vector.tensor_copy(xo_gs[:], xo_plane[:].indirect(l2[:]))
         nc.vector.tensor_copy(xo_g[:], xo_table[:].indirect(l2[:]))
-        w_dealt = [held.tile([P, 2, P], U8, name="w_dealt%d" % t, align_bytes=64) for t in range(PACK)]
-        for t in range(PACK):
-            nc.gpsimd.tensor_copy(w_dealt[t][:], w_plane[:].rearrange("p a (m t) -> p t a m", t=PACK)[:, t, :, :])
-
-        acc = [psum.tile([P, J], F32, name="acc%d" % t) for t in range(PACK)]
-        for a, (codes, scales, fmt) in enumerate(((xt_g, xt_gs, E5M2), (xo_g, xo_gs, E4M3))):
-            for t in range(PACK):
-                nc.tensor.matmul_mx(out=acc[t][:], lhsT=w_codes[a][:, t, :].bitcast(E2M1), lhsT_scale=w_dealt[t][:, a, :],
-                                    rhs=codes[:].bitcast(fmt), rhs_scale=scales[:], start=(a == 0), stop=(a == 1))
+        w_spread = held.tile([P, 2, R // 4], I32, name="w_spread", tag="xo_table")
+        for h in range(2):
+            nc.vector.tensor_copy(w_spread[64 * h : 64 * (h + 1)], w_stage[:, h])
+        w_plane = w_spread[:].bitcast(U8).rearrange("p a (m t) -> p t a m", t=PACK)
 
         hid = held.tile([P, O, PACK], BF16, name="hid", align_bytes=64)
-        a_rows = [held.tile([P, J], F32, name="a_rows%d" % t) for t in range(PACK)]
+        a_rows = []
         for t in range(PACK):
-            nc.vector.tensor_copy(a_rows[t][:], acc[t][:])
+            w_dealt = held.tile([P, 2, P], U8, name="w_dealt%d" % t, align_bytes=64)
+            nc.vector.tensor_copy(w_dealt[:], w_plane[:, t, :, :])
+            acc = psum.tile([P, J], F32, name="acc%d" % t)
+            for a, (codes, scales, fmt) in enumerate(((xt_g, xt_gs, E5M2), (xo_g, xo_gs, E4M3))):
+                nc.tensor.matmul_mx(out=acc[:], lhsT=w_codes[a][:, t, :].bitcast(E2M1), lhsT_scale=w_dealt[:, a, :],
+                                    rhs=codes[:].bitcast(fmt), rhs_scale=scales[:], start=(a == 0), stop=(a == 1))
+            a_rows.append(held.tile([P, J], F32, name="a_rows%d" % t))
+            nc.vector.tensor_copy(a_rows[t][:], acc[:])
+        hid_codes = held.tile([P, O], U32, name="hid_codes", align_bytes=64)
+        hid_scales = held.tile([P, O], U8, name="hid_scales", align_bytes=64)
+        diffs = [held.tile([P, 2, O], F32, name="diffs%d" % u) for u in range(2)]
         for t in range(PACK):
             gate = held.tile([P, O], F32, name="gate%d" % t)
             first = held.tile([P, O], F32, name="first%d" % t)
             second = held.tile([P, O], F32, name="second%d" % t)
             gated = held.tile([P, O], F32, name="gated%d" % t)
-            diff = held.tile([P, O], F32, name="diff%d" % t)
             nc.scalar.activation(out=gate[:], in_=a_rows[t][:].indirect(l4[:]), func=ACT.Sigmoid, bias=rows["bg"][:, t : t + 1], scale=rows["sg"][:, t : t + 1])
             nc.scalar.activation(out=first[:], in_=a_rows[t][:].indirect(l3[:]), func=ACT.Copy, scale=rows["sa"][:, t : t + 1])
-            nc.scalar.activation(out=second[:], in_=a_rows[t][:].indirect(l5[:]), func=ACT.Copy, scale=rows["sb"][:, t : t + 1])
             nc.vector.tensor_tensor(gated[:], first[:], gate[:], ALU.mult)
-            nc.vector.tensor_tensor(diff[:], gated[:], second[:], ALU.subtract)
-            nc.vector.scalar_tensor_tensor(hid[:, :, t], diff[:], -1.0, diff[:], ALU.mult, ALU.max)
-
-        hid_codes = held.tile([P, O], U32, name="hid_codes", align_bytes=64)
-        hid_scales = held.tile([P, O], U8, name="hid_scales", align_bytes=64)
-        nc.vector.quantize_mx(out=hid_codes[:].bitcast(E4M3), scales=hid_scales[:], in_=hid[:].rearrange("p o t -> p (o t)"))
+            parts = 2 if t == PACK - 1 else 1
+            for c in range(parts):
+                cols = slice(c * O // parts, (c + 1) * O // parts)
+                entries = slice(cols.start // 16, cols.stop // 16)
+                nc.scalar.activation(out=second[:, cols], in_=a_rows[t][:].indirect(l5[:, entries]), func=ACT.Copy, scale=rows["sb"][:, t : t + 1])
+                nc.vector.tensor_tensor(diffs[t // 2][:, t % 2, cols], gated[:, cols], second[:, cols], ALU.subtract)
+                if t % 2 == 1:
+                    pair = diffs[t // 2][:, :, cols].rearrange("p t o -> p o t")
+                    nc.vector.scalar_tensor_tensor(hid[:, cols, t - 1 : t + 1], pair, -1.0, pair, ALU.mult, ALU.max)
+                if t == PACK - 1:
+                    nc.vector.quantize_mx(out=hid_codes[:, cols].bitcast(E4M3), scales=hid_scales[:, cols], in_=hid[:, cols, :].rearrange("p o t -> p (o t)"))
 
         prod = [psum.tile([P, O], F32, name="prod%d" % h) for h in range(2)]
         p_rows = [held.tile([P, O], F32, name="p_rows%d" % h) for h in range(2)]
@@ -143,5 +152,7 @@ def tile_list_gatedless_bank_one_pagetwice_kernel(tc, xt_words, xt_scales, xo_wo
         nc.vector.tensor_tensor(sums[0][:], pages[0][0][:], pages[1][0][:], ALU.add)
         nc.sync.dma_start(out[0:P, :], sums[0][:])
         nc.vector.tensor_copy(pages[0][1][:].indirect(l6[:, :half]), p_rows[1][:, : O // 2])
-        nc.vector.tensor_tensor(sums[1][:], pages[0][1][:], pages[1][1][:], ALU.add)
-        nc.sync.dma_start(out[P : 2 * P, :], sums[1][:])
+        for c, engine in enumerate((nc.sync, nc.scalar)):
+            cols = slice(c * E // 2, (c + 1) * E // 2)
+            nc.vector.tensor_tensor(sums[1][:, cols], pages[0][1][:, cols], pages[1][1][:, cols], ALU.add)
+            engine.dma_start(out[P : 2 * P, cols], sums[1][:, cols])

@@ -36,56 +36,65 @@ def tile_list_gatedless_bank_one_pagetwice_kernel(tc, xt_words, xt_scales, xo_wo
             for r in range(PACK):
                 engine.dma_start(plane[r:P:32, :].bitcast(I32), scales[0][r:16:PACK, :].bitcast(I32))
 
-        def load_halves(engines, stage, scales):
+        def load_halves(stage, first_row, scales):
             rows4 = scales[0].bitcast(I32).rearrange("(h q r) c -> q r h c", h=2, q=2)
             for q in range(2):
-                engines[q].dma_start(stage[32 * q : 32 * q + PACK], rows4[q])
+                nc.sync.dma_start(stage[first_row + 32 * q : first_row + 32 * q + PACK], rows4[q])
 
         xt_stage = held.tile([64, 2, T // 4], I32, name="xt_stage")
-        w_stage = held.tile([64, 2, 2, R // 4], I32, name="w_stage")
+        xo_stage = held.tile([P, 2, T // 4], I32, name="xo_stage")
+        w_stage = held.tile([P, 2, 2, R // 4], I32, name="w_stage", align_bytes=64)
         xt_plane = held.tile([P, T], U8, name="xt_plane", align_bytes=64)
         xo_plane = held.tile([P, T], U8, name="xo_plane", align_bytes=64)
         wb_plane = held.tile([P, N], U8, name="wb_plane", align_bytes=64)
-        nc.vector.memset(xt_stage[:], 0)
-        nc.vector.memset(xo_plane[:].bitcast(I32), 0)
-        nc.vector.memset(w_stage[:], 0)
+        for stage in (xt_stage[:], xo_stage[64:P]):
+            nc.vector.memset(stage[:, 0, :], 0)
+            nc.gpsimd.memset(stage[:, 1, :], 0)
+        nc.vector.memset(w_stage[0:64], 0)
         nc.vector.memset(wb_plane[:].bitcast(I32), 0)
 
         xt_table = held.tile([P, T], U32, name="xt_table")
-        xo_table = held.tile([P, T], U32, name="xo_table", tag="xo_table")
+        xo_table = held.tile([P, T], U32, name="xo_table")
         w_raw = held.tile([P, 2 * R], U8, name="w_raw")
         w0_raw = held.tile([P, 2 * R], U8, name="w0_raw")
-        nc.scalar.dma_start(w_raw[:].bitcast(I32), w_words[0].bitcast(I32))
-        nc.scalar.dma_start(w0_raw[:].bitcast(I32), w0_words[0].bitcast(I32))
-        nc.scalar.dma_start(xt_table[:].bitcast(I32), xt_words[0].rearrange("p n t -> p (n t)").bitcast(I32))
         l1 = load_list(offs, "l1")
         l2 = load_list(offs2, "l2")
-        l4 = load_list(offs4, "l4")
-        load_halves((nc.sync, nc.sync), xt_stage[:], xt_scales)
-        load_rows(nc.sync, xo_plane, xo_scales)
+        load_halves(xt_stage[:], 0, xt_scales)
+        load_halves(xo_stage[:], 64, xo_scales)
+        nc.sync.dma_start(xt_table[:].bitcast(I32), xt_words[0].rearrange("p n t -> p (n t)").bitcast(I32))
         nc.sync.dma_start(xo_table[:].bitcast(I32), xo_words[0].rearrange("p n t -> p (n t)").bitcast(I32))
-        load_halves((nc.sync, nc.sync), w_stage[:, :, 0, :], w_scales)
-        load_halves((nc.sync, nc.sync), w_stage[:, :, 1, :], w0_scales)
-        l3 = load_list(offs3, "l3")
-        l5 = load_list(offs5, "l5")
+        load_halves(w_stage[:, :, 0, :], 0, w_scales)
+        load_halves(w_stage[:, :, 1, :], 0, w0_scales)
+        nc.sync.dma_start(w_raw[:].bitcast(I32), w_words[0].bitcast(I32))
+        nc.sync.dma_start(w0_raw[:].bitcast(I32), w0_words[0].bitcast(I32))
         rows = {}
-        for name, src in (("sg", sg), ("bg", bg), ("sa", sa), ("sb", sb)):
+        def load_column(name, src):
             rows[name] = held.tile([P, PACK], F32, name=name)
-            nc.gpsimd.dma_start(rows[name][:], src.rearrange("(p t) one -> p (t one)", t=PACK))
+            nc.sync.dma_start(rows[name][:], src.rearrange("(p t) one -> p (t one)", t=PACK))
+        l4 = load_list(offs4, "l4")
+        load_column("sg", sg)
+        load_column("bg", bg)
+        l3 = load_list(offs3, "l3")
+        load_column("sa", sa)
+        l5 = load_list(offs5, "l5")
+        load_column("sb", sb)
         wb_codes = held.tile([P, 2 * N], U8, name="wb_codes", align_bytes=64)
-        l6 = load_list(offs6, "l6")
-        l7 = load_list(offs7, "l7")
         nc.sync.dma_start(wb_codes[:].bitcast(I32), wb_words[0].bitcast(I32))
         load_rows(nc.sync, wb_plane, wb_scales)
+        l6 = load_list(offs6, "l6")
+        l7 = load_list(offs7, "l7")
 
         pages = [[held.tile([P, E], F32, name="page%d%d" % (a, h)) for h in range(2)] for a in range(2)]
         for a in range(2):
             for h in range(2):
                 nc.vector.memset(pages[a][h][:], 0.0)
 
-        w_codes = [held.tile([P, PACK, 2 * P], U8, name="w_codes%d" % a, align_bytes=64) for a in range(2)]
-        for a, raw in enumerate((w_raw, w0_raw)):
-            nc.scalar.copy(w_codes[a][:].bitcast(U16), raw[:].bitcast(U16).rearrange("p (m t) -> p t m", t=PACK))
+        w_first = [held.tile([P, 1, 2 * P], U8, name="w_first%d" % a, align_bytes=64) for a in range(2)]
+        w_rest = [held.tile([P, PACK - 1, 2 * P], U8, name="w_rest%d" % a, align_bytes=64) for a in range(2)]
+        for tiles, slices in ((w_first, slice(0, 1)), (w_rest, slice(1, PACK))):
+            for a, raw in enumerate((w_raw, w0_raw)):
+                nc.scalar.copy(tiles[a][:].bitcast(U16), raw[:].bitcast(U16).rearrange("p (m t) -> p t m", t=PACK)[:, slices, :])
+        w_codes = [[w_first[a][:, 0, :]] + [w_rest[a][:, u, :] for u in range(PACK - 1)] for a in range(2)]
 
         xt_gs = held.tile([P, J], U8, name="xt_gs", align_bytes=64)
         xo_gs = held.tile([P, J], U8, name="xo_gs", align_bytes=64)
@@ -94,13 +103,13 @@ def tile_list_gatedless_bank_one_pagetwice_kernel(tc, xt_words, xt_scales, xo_wo
         for h in range(2):
             nc.vector.tensor_copy(xt_plane[64 * h : 64 * (h + 1), :].bitcast(I32), xt_stage[:, h, :])
         nc.vector.tensor_copy(xt_gs[:], xt_plane[:].indirect(l1[:]))
-        nc.vector.tensor_copy(xt_g[:], xt_table[:].indirect(l1[:]))
+        for h in (1, 0):
+            nc.vector.tensor_copy(xo_plane[64 * h : 64 * (h + 1), :].bitcast(I32), xo_stage[64:P, h, :])
         nc.vector.tensor_copy(xo_gs[:], xo_plane[:].indirect(l2[:]))
+        nc.vector.tensor_copy(xt_g[:], xt_table[:].indirect(l1[:]))
         nc.vector.tensor_copy(xo_g[:], xo_table[:].indirect(l2[:]))
-        w_spread = held.tile([P, 2, R // 4], I32, name="w_spread", tag="xo_table")
-        for h in range(2):
-            nc.vector.tensor_copy(w_spread[64 * h : 64 * (h + 1)], w_stage[:, h])
-        w_plane = w_spread[:].bitcast(U8).rearrange("p a (m t) -> p t a m", t=PACK)
+        nc.vector.tensor_copy(w_stage[64:P, 0, :, :].rearrange("p a c -> p (a c)"), w_stage[0:64, 1, :, :].rearrange("p a c -> p (a c)"))
+        w_plane = w_stage[:, 0, :, :].bitcast(U8).rearrange("p a (m t) -> p t a m", t=PACK)
 
         hid = held.tile([P, O, PACK], BF16, name="hid", align_bytes=64)
         a_rows = []
@@ -108,14 +117,14 @@ def tile_list_gatedless_bank_one_pagetwice_kernel(tc, xt_words, xt_scales, xo_wo
             w_dealt = held.tile([P, 2, P], U8, name="w_dealt%d" % t, align_bytes=64)
             nc.vector.tensor_copy(w_dealt[:], w_plane[:, t, :, :])
             acc = psum.tile([P, J], F32, name="acc%d" % t)
-            for a, (codes, scales, fmt) in enumerate(((xt_g, xt_gs, E5M2), (xo_g, xo_gs, E4M3))):
-                nc.tensor.matmul_mx(out=acc[:], lhsT=w_codes[a][:, t, :].bitcast(E2M1), lhsT_scale=w_dealt[:, a, :],
-                                    rhs=codes[:].bitcast(fmt), rhs_scale=scales[:], start=(a == 0), stop=(a == 1))
+            for a, codes, scales, fmt in ((1, xo_g, xo_gs, E4M3), (0, xt_g, xt_gs, E5M2)):
+                nc.tensor.matmul_mx(out=acc[:], lhsT=w_codes[a][t].bitcast(E2M1), lhsT_scale=w_dealt[:, a, :],
+                                    rhs=codes[:].bitcast(fmt), rhs_scale=scales[:], start=(a == 1), stop=(a == 0))
             a_rows.append(held.tile([P, J], F32, name="a_rows%d" % t))
             nc.vector.tensor_copy(a_rows[t][:], acc[:])
         hid_codes = held.tile([P, O], U32, name="hid_codes", align_bytes=64)
         hid_scales = held.tile([P, O], U8, name="hid_scales", align_bytes=64)
-        diffs = [held.tile([P, 2, O], F32, name="diffs%d" % u) for u in range(2)]
+        diff = held.tile([P, PACK, O], F32, name="diff")
         for t in range(PACK):
             gate = held.tile([P, O], F32, name="gate%d" % t)
             first = held.tile([P, O], F32, name="first%d" % t)
@@ -129,12 +138,11 @@ def tile_list_gatedless_bank_one_pagetwice_kernel(tc, xt_words, xt_scales, xo_wo
                 cols = slice(c * O // parts, (c + 1) * O // parts)
                 entries = slice(cols.start // 16, cols.stop // 16)
                 nc.scalar.activation(out=second[:, cols], in_=a_rows[t][:].indirect(l5[:, entries]), func=ACT.Copy, scale=rows["sb"][:, t : t + 1])
-                nc.vector.tensor_tensor(diffs[t // 2][:, t % 2, cols], gated[:, cols], second[:, cols], ALU.subtract)
-                if t % 2 == 1:
-                    pair = diffs[t // 2][:, :, cols].rearrange("p t o -> p o t")
-                    nc.vector.scalar_tensor_tensor(hid[:, cols, t - 1 : t + 1], pair, -1.0, pair, ALU.mult, ALU.max)
-                if t == PACK - 1:
-                    nc.vector.quantize_mx(out=hid_codes[:, cols].bitcast(E4M3), scales=hid_scales[:, cols], in_=hid[:, cols, :].rearrange("p o t -> p (o t)"))
+                nc.vector.tensor_tensor(diff[:, t, cols], gated[:, cols], second[:, cols], ALU.subtract)
+        for c in range(2):
+            cols = slice(c * O // 2, (c + 1) * O // 2)
+            nc.scalar.activation(out=hid[:, cols, :], in_=diff[:, :, cols].rearrange("p t o -> p o t"), func=ACT.Abs)
+            nc.vector.quantize_mx(out=hid_codes[:, cols].bitcast(E4M3), scales=hid_scales[:, cols], in_=hid[:, cols, :].rearrange("p o t -> p (o t)"))
 
         prod = [psum.tile([P, O], F32, name="prod%d" % h) for h in range(2)]
         p_rows = [held.tile([P, O], F32, name="p_rows%d" % h) for h in range(2)]

from contextlib import ExitStack

import concourse.mybir as mybir

F32 = mybir.dt.float32
BF16 = mybir.dt.bfloat16
I32 = mybir.dt.int32
U32 = mybir.dt.uint32
U16 = mybir.dt.uint16
U8 = mybir.dt.uint8
E4M3 = mybir.dt.float8_e4m3fn_x4
E5M2 = mybir.dt.float8_e5m2_x4
E2M1 = mybir.dt.float4_e2m1fn_x4
ACT = mybir.ActivationFunctionType
ALU = mybir.AluOpType

P = 128
PACK = 4
QUADS = 4
T, J, R, O, N, E = 1024, 256, 512, 128, 256, 512
FLOPS = 2 * (2 * 512 * R * J + R * N * O)


def tile_list_gatedless_bank_one_pagetwice_kernel(tc, xt_words, xt_scales, xo_words, xo_scales, w_words, w_scales, w0_words, w0_scales, sa, sb, sg, bg, wb_words, wb_scales, offs, offs2, offs3, offs4, offs5, offs6, offs7, out):
    nc = tc.nc
    with ExitStack() as ctx:
        held = ctx.enter_context(tc.tile_pool(name="held", bufs=1))
        psum = ctx.enter_context(tc.psum_pool(name="psum", bufs=1))

        def load_list(src, name):
            tile = held.tile(list(src.shape), U16, name=name)
            nc.sync.dma_start(tile[:], src)
            return tile

        def load_rows(engine, plane, scales):
            for r in range(PACK):
                engine.dma_start(plane[r:P:32, :].bitcast(I32), scales[0][r:16:PACK, :].bitcast(I32))

        def load_halves(stage, first_row, scales):
            rows4 = scales[0].bitcast(I32).rearrange("(h q r) c -> q r h c", h=2, q=2)
            for q in range(2):
                nc.sync.dma_start(stage[first_row + 32 * q : first_row + 32 * q + PACK], rows4[q])

        xt_stage = held.tile([64, 2, T // 4], I32, name="xt_stage")
        xo_stage = held.tile([P, 2, T // 4], I32, name="xo_stage")
        w_stage = held.tile([P, 2, 2, R // 4], I32, name="w_stage", align_bytes=64)
        xt_plane = held.tile([P, T], U8, name="xt_plane", align_bytes=64)
        xo_plane = held.tile([P, T], U8, name="xo_plane", align_bytes=64)
        wb_plane = held.tile([P, N], U8, name="wb_plane", align_bytes=64)
        for stage in (xt_stage[:], xo_stage[64:P]):
            nc.vector.memset(stage[:, 0, :], 0)
            nc.gpsimd.memset(stage[:, 1, :], 0)
        nc.vector.memset(w_stage[0:64], 0)
        nc.vector.memset(wb_plane[:].bitcast(I32), 0)

        xt_table = held.tile([P, T], U32, name="xt_table")
        xo_table = held.tile([P, T], U32, name="xo_table")
        w_raw = held.tile([P, 2 * R], U8, name="w_raw")
        w0_raw = held.tile([P, 2 * R], U8, name="w0_raw")
        l1 = load_list(offs, "l1")
        l2 = load_list(offs2, "l2")
        load_halves(xt_stage[:], 0, xt_scales)
        load_halves(xo_stage[:], 64, xo_scales)
        nc.sync.dma_start(xt_table[:].bitcast(I32), xt_words[0].rearrange("p n t -> p (n t)").bitcast(I32))
        nc.sync.dma_start(xo_table[:].bitcast(I32), xo_words[0].rearrange("p n t -> p (n t)").bitcast(I32))
        load_halves(w_stage[:, :, 0, :], 0, w_scales)
        load_halves(w_stage[:, :, 1, :], 0, w0_scales)
        nc.sync.dma_start(w_raw[:].bitcast(I32), w_words[0].bitcast(I32))
        nc.sync.dma_start(w0_raw[:].bitcast(I32), w0_words[0].bitcast(I32))
        rows = {}
        def load_column(name, src):
            rows[name] = held.tile([P, PACK], F32, name=name)
            nc.sync.dma_start(rows[name][:], src.rearrange("(p t) one -> p (t one)", t=PACK))
        l4 = load_list(offs4, "l4")
        load_column("sg", sg)
        load_column("bg", bg)
        l3 = load_list(offs3, "l3")
        load_column("sa", sa)
        l5 = load_list(offs5, "l5")
        load_column("sb", sb)
        wb_codes = held.tile([P, 2 * N], U8, name="wb_codes", align_bytes=64)
        nc.sync.dma_start(wb_codes[:].bitcast(I32), wb_words[0].bitcast(I32))
        load_rows(nc.sync, wb_plane, wb_scales)
        l6 = load_list(offs6, "l6")
        l7 = load_list(offs7, "l7")

        pages = [[held.tile([P, E], F32, name="page%d%d" % (a, h)) for h in range(2)] for a in range(2)]
        for a in range(2):
            for h in range(2):
                nc.vector.memset(pages[a][h][:], 0.0)

        w_first = [held.tile([P, 1, 2 * P], U8, name="w_first%d" % a, align_bytes=64) for a in range(2)]
        w_rest = [held.tile([P, PACK - 1, 2 * P], U8, name="w_rest%d" % a, align_bytes=64) for a in range(2)]
        for tiles, slices in ((w_first, slice(0, 1)), (w_rest, slice(1, PACK))):
            for a, raw in enumerate((w_raw, w0_raw)):
                nc.scalar.copy(tiles[a][:].bitcast(U16), raw[:].bitcast(U16).rearrange("p (m t) -> p t m", t=PACK)[:, slices, :])
        w_codes = [[w_first[a][:, 0, :]] + [w_rest[a][:, u, :] for u in range(PACK - 1)] for a in range(2)]

        xt_gs = held.tile([P, J], U8, name="xt_gs", align_bytes=64)
        xo_gs = held.tile([P, J], U8, name="xo_gs", align_bytes=64)
        xt_g = held.tile([P, J], U32, name="xt_g", align_bytes=64)
        xo_g = held.tile([P, J], U32, name="xo_g", align_bytes=64)
        for h in range(2):
            nc.vector.tensor_copy(xt_plane[64 * h : 64 * (h + 1), :].bitcast(I32), xt_stage[:, h, :])
        nc.vector.tensor_copy(xt_gs[:], xt_plane[:].indirect(l1[:]))
        for h in (1, 0):
            nc.vector.tensor_copy(xo_plane[64 * h : 64 * (h + 1), :].bitcast(I32), xo_stage[64:P, h, :])
        nc.vector.tensor_copy(xo_gs[:], xo_plane[:].indirect(l2[:]))
        nc.vector.tensor_copy(xt_g[:], xt_table[:].indirect(l1[:]))
        nc.vector.tensor_copy(xo_g[:], xo_table[:].indirect(l2[:]))
        nc.vector.tensor_copy(w_stage[64:P, 0, :, :].rearrange("p a c -> p (a c)"), w_stage[0:64, 1, :, :].rearrange("p a c -> p (a c)"))
        w_plane = w_stage[:, 0, :, :].bitcast(U8).rearrange("p a (m t) -> p t a m", t=PACK)

        hid = held.tile([P, O, PACK], BF16, name="hid", align_bytes=64)
        a_rows = []
        for t in range(PACK):
            w_dealt = held.tile([P, 2, P], U8, name="w_dealt%d" % t, align_bytes=64)
            nc.vector.tensor_copy(w_dealt[:], w_plane[:, t, :, :])
            acc = psum.tile([P, J], F32, name="acc%d" % t)
            for a, codes, scales, fmt in ((1, xo_g, xo_gs, E4M3), (0, xt_g, xt_gs, E5M2)):
                nc.tensor.matmul_mx(out=acc[:], lhsT=w_codes[a][t].bitcast(E2M1), lhsT_scale=w_dealt[:, a, :],
                                    rhs=codes[:].bitcast(fmt), rhs_scale=scales[:], start=(a == 1), stop=(a == 0))
            a_rows.append(held.tile([P, J], F32, name="a_rows%d" % t))
            nc.vector.tensor_copy(a_rows[t][:], acc[:])
        hid_codes = held.tile([P, O], U32, name="hid_codes", align_bytes=64)
        hid_scales = held.tile([P, O], U8, name="hid_scales", align_bytes=64)
        diff = held.tile([P, PACK, O], F32, name="diff")
        for t in range(PACK):
            gate = held.tile([P, O], F32, name="gate%d" % t)
            first = held.tile([P, O], F32, name="first%d" % t)
            second = held.tile([P, O], F32, name="second%d" % t)
            gated = held.tile([P, O], F32, name="gated%d" % t)
            nc.scalar.activation(out=gate[:], in_=a_rows[t][:].indirect(l4[:]), func=ACT.Sigmoid, bias=rows["bg"][:, t : t + 1], scale=rows["sg"][:, t : t + 1])
            nc.scalar.activation(out=first[:], in_=a_rows[t][:].indirect(l3[:]), func=ACT.Copy, scale=rows["sa"][:, t : t + 1])
            nc.vector.tensor_tensor(gated[:], first[:], gate[:], ALU.mult)
            parts = 2 if t == PACK - 1 else 1
            for c in range(parts):
                cols = slice(c * O // parts, (c + 1) * O // parts)
                entries = slice(cols.start // 16, cols.stop // 16)
                nc.scalar.activation(out=second[:, cols], in_=a_rows[t][:].indirect(l5[:, entries]), func=ACT.Copy, scale=rows["sb"][:, t : t + 1])
                nc.vector.tensor_tensor(diff[:, t, cols], gated[:, cols], second[:, cols], ALU.subtract)
        for c in range(2):
            cols = slice(c * O // 2, (c + 1) * O // 2)
            nc.scalar.activation(out=hid[:, cols, :], in_=diff[:, :, cols].rearrange("p t o -> p o t"), func=ACT.Abs)
            nc.vector.quantize_mx(out=hid_codes[:, cols].bitcast(E4M3), scales=hid_scales[:, cols], in_=hid[:, cols, :].rearrange("p o t -> p (o t)"))

        prod = [psum.tile([P, O], F32, name="prod%d" % h) for h in range(2)]
        p_rows = [held.tile([P, O], F32, name="p_rows%d" % h) for h in range(2)]
        for h in range(2):
            nc.tensor.matmul_mx(out=prod[h][:], lhsT=wb_codes[:, 2 * P * h : 2 * P * (h + 1)].bitcast(E2M1), lhsT_scale=wb_plane[:, P * h : P * (h + 1)],
                                rhs=hid_codes[:].bitcast(E4M3), rhs_scale=hid_scales[:], start=True, stop=True)
        nc.vector.tensor_copy(p_rows[0][:], prod[0][:])
        nc.scalar.copy(p_rows[1][:], prod[1][:])
        sums = [held.tile([P, E], F32, name="sums%d" % h) for h in range(2)]
        half = O // 32
        nc.vector.tensor_copy(pages[0][0][:].indirect(l6[:]), p_rows[0][:])
        nc.scalar.activation(out=pages[1][0][:].indirect(l7[:]), in_=p_rows[0][:], func=ACT.Copy)
        nc.scalar.activation(out=pages[0][1][:].indirect(l6[:, half:]), in_=p_rows[1][:, O // 2 :], func=ACT.Copy)
        nc.scalar.activation(out=pages[1][1][:].indirect(l7[:]), in_=p_rows[1][:], func=ACT.Copy)
        nc.vector.tensor_tensor(sums[0][:], pages[0][0][:], pages[1][0][:], ALU.add)
        nc.sync.dma_start(out[0:P, :], sums[0][:])
        nc.vector.tensor_copy(pages[0][1][:].indirect(l6[:, :half]), p_rows[1][:, : O // 2])
        for c, engine in enumerate((nc.sync, nc.scalar)):
            cols = slice(c * E // 2, (c + 1) * E // 2)
            nc.vector.tensor_tensor(sums[1][:, cols], pages[0][1][:, cols], pages[1][1][:, cols], ALU.add)
            engine.dma_start(out[P : 2 * P, cols], sums[1][:, cols])
